import numpy as np
import ml_dtypes


def mxq(x, axis, fmt="e4m3"):
    dtype, down = {"e4m3": (ml_dtypes.float8_e4m3fn, 7), "e5m2": (ml_dtypes.float8_e5m2, 14)}[fmt]
    v = np.moveaxis(np.asarray(x, np.float32).astype(ml_dtypes.bfloat16).astype(np.float64), axis, -1)
    blocks = v.reshape(v.shape[:-1] + (-1, 32))
    amax = np.abs(blocks).max(-1, keepdims=True)
    byte = np.maximum(np.where(amax > 0, np.frexp(amax)[1] - 1 + 127, 0) - down, 1)
    scale = np.exp2(byte - 127.0)
    codes = (blocks / scale).astype(np.float32).astype(dtype).astype(np.float64)
    return np.moveaxis((codes * scale).reshape(v.shape), -1, axis)


WIDE = False


def mx_kscale(k):
    if not WIDE:
        return np.ones(k)
    levels = np.array([10, -10, 5, -5, 0])
    if k % 512:
        return np.exp2(np.random.permutation(np.resize(levels, k // 32))).repeat(32)
    a = np.empty((k // 512, 16))
    for p in range(k // 512):
        a[p, :8] = np.random.permutation(np.resize(levels, 8))
        for g in range(8):
            far = levels[np.abs(levels - a[p, g]) >= 10]
            a[p, g + 8] = far[np.random.randint(len(far))]
    return np.exp2(a.ravel()).repeat(32)


def f64(x):
    return np.asarray(x).astype(np.float64)


def striped8(idx):
    return np.asarray(idx).reshape(8, -1, 16).transpose(0, 2, 1).reshape(128, -1).astype(np.uint16)


def unstriped8(offs):
    return offs.reshape(8, 16, -1).transpose(0, 2, 1).reshape(8, -1).astype(np.int64)


def pick8(x, idx, run):
    r = np.arange(len(x))
    return x[r[:, None], idx[r % (8 * run) // run]]


def bf(x):
    return np.asarray(x, np.float32).astype(ml_dtypes.bfloat16)


def planes(Y):
    r, m = Y.shape
    b = f64(bf(Y)).reshape(r // 32, 32, m)
    amax = np.abs(b).max(1)
    byte = np.clip(np.where(amax > 0, np.frexp(amax)[1] - 1 + 127 - 7, 1), 1, 254)
    codes = (b * np.exp2(127.0 - byte)[:, None, :]).reshape(r, m).astype(np.float32).astype(ml_dtypes.float8_e4m3fn).view(np.uint8)
    words = codes.reshape(r // 512, 128, 4, m).transpose(0, 1, 3, 2)
    return np.ascontiguousarray(words), np.ascontiguousarray(byte.astype(np.uint8).reshape(r // 512, 16, m))


D, T, I, E = 512, 1024, 512, 512


def setup_inputs():
    n = np.random.standard_normal
    idx = np.stack([np.random.permutation(T)[:I] for _ in range(8)])
    fd = mx_kscale(D)
    fi = mx_kscale(I)
    return {
        "state": (n((D, E)) * (np.arange(D)[:, None] // 64 == np.arange(E) // 64) * 0.125 * fd[:, None]).astype(np.float32),
        "keys": (n((D, T)) / fd[:, None]).astype(np.float32),
        "vals": (n((E, T))).astype(np.float32),
        "step": (np.random.uniform(0.05, 0.2, (I, 1)) * fi[:, None]).astype(np.float32),
        "esc": (np.random.uniform(0.5, 2.0, (I, 1)) / fi[:, None]).astype(np.float32),
        "dsc": (np.random.uniform(0.5, 2.0, (1, D)) * fd).astype(np.float32),
        "own": ((np.arange(D)[:, None] // 64 == np.arange(E) // 64) + 0.0).astype(np.float32),
        "offs": striped8(idx),
    }


def reference(state, keys, vals, step, esc, dsc, own, offs):
    idx = unstriped8(offs)
    stateq = mxq(f64(state), 0, "e4m3")
    keysidxq = mxq(pick8(f64(keys), idx, 64), 0, "e4m3")
    b = stateq.T @ keysidxq
    err = pick8(f64(vals), idx, 64) - b
    et = err.T
    es = et * f64(esc)
    kt = pick8(f64(keys), idx, 64).T
    ks = kt * f64(step) * f64(dsc)
    ksq = mxq(ks, 0, "e4m3")
    esq = mxq(es, 0, "e4m3")
    s = ksq.T @ esq
    y = s * f64(own)
    words, scales = planes(y)
    return y, words, scales

@@ -1,0 +1,168 @@
+from contextlib import ExitStack
+
+import concourse.mybir as mybir
+from concourse.masks import make_identity
+
+D, T, I, E = 512, 1024, 512, 512
+FLOPS = 2 * D * E * I * 2
+
+F32 = mybir.dt.float32
+BF16 = mybir.dt.bfloat16
+I32 = mybir.dt.int32
+U32 = mybir.dt.uint32
+U16 = mybir.dt.uint16
+U8 = mybir.dt.uint8
+FP8X4 = mybir.dt.float8_e4m3fn_x4
+MULT = mybir.AluOpType.mult
+COPY = mybir.ActivationFunctionType.Copy
+
+P = 128
+PACK = 4
+QUARTERS = 4
+QW = E // QUARTERS
+
+
+def tile_attend_ownlists_delta_pl_kernel(tc, state, keys, vals, step, esc, dsc, own, offs, out_0, out_1, out_2):
+    nc = tc.nc
+    with ExitStack() as ctx:
+        sb = ctx.enter_context(tc.tile_pool(name="sb", bufs=1))
+        ps = ctx.enter_context(tc.psum_pool(name="ps", bufs=1))
+
+        def bank(n, name):
+            return ps.tile([P, PACK, P], F32, name=name, tag="bank%d" % n)
+
+        def quantize(codes, scales, values):
+            nc.vector.quantize_mx(out=codes.bitcast(FP8X4), scales=scales, in_=values)
+
+        def mx(out, lhs, lhs_scale, rhs, rhs_scale):
+            nc.tensor.matmul_mx(out=out, lhsT=lhs.bitcast(FP8X4), lhsT_scale=lhs_scale,
+                                rhs=rhs.bitcast(FP8X4), rhs_scale=rhs_scale, start=True, stop=True)
+
+        keys_planes = keys.rearrange("(p t) n -> p t n", t=PACK)
+        vals_planes = vals.rearrange("(p t) n -> p t n", t=PACK)
+        state_planes = state.rearrange("(p t) e -> p t e", t=PACK)
+
+        offsets = sb.tile([P, I // 16], U16, name="offsets")
+        nc.sync.dma_start(offsets[:], offs)
+        step4 = sb.tile([P, PACK], F32, name="step4")
+        dsc4 = sb.tile([P, PACK], F32, name="dsc4")
+        esc4 = sb.tile([P, PACK], F32, name="esc4")
+        nc.scalar.dma_start(step4[:], step.rearrange("(s r) o -> s (r o)", r=PACK))
+        nc.scalar.dma_start(dsc4[:], dsc.rearrange("o (p t) -> (o p) t", t=PACK))
+        nc.scalar.dma_start(esc4[:], esc.rearrange("(s r) o -> s (r o)", r=PACK))
+
+        key_pool = [sb.tile([P, T], F32, name="key_pool%d" % t) for t in range(PACK)]
+        val_pool = [sb.tile([P, T], F32, name="val_pool%d" % t) for t in range(PACK)]
+        state_raw = sb.tile([P, PACK, E], F32, name="state_raw")
+        own_sb = sb.tile([P, PACK, E], F32, name="own_sb")
+        state_parts = [slice(0, 1), slice(1, 2), slice(2, 4)]
+        for t in range(PACK):
+            nc.sync.dma_start(key_pool[t][:], keys_planes[:, t, :])
+            if t < len(state_parts):
+                nc.sync.dma_start(state_raw[:, state_parts[t], :], state_planes[:, state_parts[t], :])
+        for t in range(PACK):
+            nc.sync.dma_start(val_pool[t][:], vals_planes[:, t, :])
+        nc.sync.dma_start(own_sb[:], own.rearrange("(p t) e -> p t e", t=PACK))
+
+        ident = sb.tile([P, P], F32, name="ident")
+        make_identity(nc, ident[:])
+
+        step_rows = bank(0, "step_rows")
+        for r in range(PACK):
+            nc.tensor.transpose(step_rows[:, r, :], step4[:, r:r + 1].to_broadcast([P, P]), ident[:])
+
+        kg = sb.tile([P, PACK, I], F32, name="kg")
+        ks_rows = [sb.tile([P, I], BF16, name="ks_rows%d" % t, align_bytes=64) for t in range(PACK)]
+        ks_bf = sb.tile([P, D * PACK], BF16, name="ks_bf", align_bytes=64)
+        ks_words = ks_bf[:].bitcast(F32).rearrange("s (t p u) -> s t p u", t=PACK, u=2)
+        for pair in range(2):
+            ks_turned = bank(1, "ks_turned%d" % pair)
+            for t in (2 * pair, 2 * pair + 1):
+                nc.vector.tensor_copy(kg[:, t, :], key_pool[t][:].indirect(offsets[:]))
+                nc.vector.scalar_tensor_tensor(
+                    out=ks_rows[t][:].rearrange("p (s r) -> p s r", r=PACK),
+                    in0=kg[:, t, :].rearrange("p (s r) -> p s r", r=PACK),
+                    scalar=dsc4[:, t:t + 1],
+                    in1=step_rows[:].rearrange("p r s -> p s r"),
+                    op0=MULT, op1=MULT)
+                words = ks_rows[t][:].bitcast(F32)
+                for u in range(2):
+                    nc.tensor.transpose(ks_turned[:, 2 * (t % 2) + u, :], words[:, u:I // 2:2], ident[:])
+            nc.scalar.copy(ks_words[:, 2 * pair:2 * pair + 2, :, :],
+                           ks_turned[:].rearrange("s (t u) p -> s t p u", u=2))
+
+        state_bf = sb.tile([P, E * PACK], BF16, name="state_bf", align_bytes=64)
+        nc.scalar.copy(state_bf[:].rearrange("p (t m j) -> p m j t", t=PACK, j=PACK),
+                       state_raw[:].rearrange("p j (m t) -> p m j t", t=PACK))
+        state_codes = sb.tile([P, E], U32, name="state_codes", align_bytes=64)
+        state_scales = sb.tile([P, E], U8, name="state_scales", align_bytes=64)
+        quantize(state_codes[:], state_scales[:], state_bf[:])
+
+        key_bf = sb.tile([P, I * PACK], BF16, name="key_bf", align_bytes=64)
+        nc.scalar.copy(key_bf[:].rearrange("p (c i t) -> p c t i", t=PACK, i=4),
+                       kg[:].rearrange("p t (c i) -> p c t i", i=4))
+        key_codes = sb.tile([P, I], U32, name="key_codes", align_bytes=64)
+        key_scales = sb.tile([P, I], U8, name="key_scales", align_bytes=64)
+        quantize(key_codes[:], key_scales[:], key_bf[:])
+
+        ks_codes = sb.tile([P, D], U32, name="ks_codes", align_bytes=64)
+        ks_scales = sb.tile([P, D], U8, name="ks_scales", align_bytes=64)
+        quantize(ks_codes[:], ks_scales[:], ks_bf[:])
+
+        es_bf = sb.tile([P, QUARTERS, PACK, QW // PACK, PACK], BF16, name="es_bf", align_bytes=64)
+        esc_spread = esc4[:].unsqueeze(1).unsqueeze(1).to_broadcast([P, QUARTERS, QW // PACK, PACK])
+        for t in range(PACK):
+            vg = sb.tile([P, I], F32, name="vg%d" % t)
+            nc.vector.tensor_copy(vg[:], val_pool[t][:].indirect(offsets[:]))
+            pred = bank(2 + t % 2, "pred%d" % t)
+            cols = slice(P * t, P * (t + 1))
+            mx(pred[:].rearrange("p a b -> p (a b)"), state_codes[:, cols], state_scales[:, cols],
+               key_codes[:], key_scales[:])
+            neg_pred = sb.tile([P, PACK, P], F32, name="neg_pred%d" % t)
+            nc.scalar.activation(neg_pred[:],
+                                 pred[:].rearrange("p a b -> p (a b)").rearrange("p (s r) -> p r s", r=PACK),
+                                 COPY, scale=-1.0)
+            err = bank(4 + t, "err%d" % t)
+            vals_first = t < 2
+            sides = [[vg[:, r:I:PACK] for r in range(PACK)], [neg_pred[:, r, :] for r in range(PACK)]]
+            if not vals_first:
+                sides = sides[::-1]
+            for k in range(2):
+                for r in range(PACK):
+                    nc.tensor.matmul(err[:, r, :], sides[k][r], ident[:], is_transpose=True,
+                                     start=(k == 0 and r == 0), stop=(k == 1 and r == PACK - 1))
+            nc.vector.tensor_tensor(es_bf[:, :, t, :, :],
+                                    err[:].rearrange("s r (q c) -> s q c r", q=QUARTERS),
+                                    esc_spread, MULT)
+
+        es_codes = sb.tile([P, E], U32, name="es_codes", align_bytes=64)
+        es_scales = sb.tile([P, E], U8, name="es_scales", align_bytes=64)
+        y_codes = sb.tile([P, E], U32, name="y_codes", align_bytes=64)
+        y_scales = sb.tile([P, E], U8, name="y_scales", align_bytes=64)
+        out_rows = out_0.rearrange("(p t) e -> p t e", t=PACK)
+        out_words = out_1.rearrange("z p c r -> p (z c r)").bitcast(I32)
+        for q in range(QUARTERS):
+            cols = slice(QW * q, QW * (q + 1))
+            quantize(es_codes[:, cols], es_scales[:, cols], es_bf[:, q].rearrange("s t c r -> s (t c r)"))
+        for q in range(QUARTERS):
+            cols = slice(QW * q, QW * (q + 1))
+            upd = bank(q, "upd%d" % q)
+            for t in range(PACK):
+                rows = slice(P * t, P * (t + 1))
+                mx(upd[:, t, :], ks_codes[:, rows], ks_scales[:, rows], es_codes[:, cols], es_scales[:, cols])
+            y = sb.tile([P, PACK, QW], F32, name="y%d" % q)
+            nc.vector.tensor_tensor(y[:].rearrange("p t (c j) -> p t c j", j=PACK),
+                                    upd[:].rearrange("p t (j c) -> p t c j", j=PACK),
+                                    own_sb[:, :, cols].rearrange("p t (c j) -> p t c j", j=PACK), MULT)
+            nc.sync.dma_start(out_rows[:, :, cols], y[:])
+            y_bf = sb.tile([P, QW * PACK], BF16, name="y_bf%d" % q, align_bytes=64)
+            nc.scalar.copy(y_bf[:].rearrange("p (c i t) -> p c t i", t=PACK, i=4),
+                           y[:].rearrange("p t (c i) -> p c t i", i=4))
+            quantize(y_codes[:, cols], y_scales[:, cols], y_bf[:])
+            if q % 2 == 1:
+                half = slice(QW * (q - 1), QW * (q + 1))
+                nc.scalar.dma_start(out_words[:, half], y_codes[:, half].bitcast(I32))
+        out_scales = out_2.rearrange("z q c -> (z q) c").bitcast(I32)
+        for quad in range(4):
+            eng = nc.sync if quad % 2 == 0 else nc.scalar
+            eng.dma_start(out_scales[4 * quad:4 * quad + 4, :], y_scales[32 * quad:32 * quad + 4, :].bitcast(I32))

@@ -43,7 +43,6 @@ def tile_attend_ownlists_delta_pl_kernel(tc, state, keys, vals, step, esc, dsc, 
         state_planes = state.rearrange("(p t) e -> p t e", t=PACK)
 
         offsets = sb.tile([P, I // 16], U16, name="offsets")
-        nc.sync.dma_start(offsets[:], offs)
         step4 = sb.tile([P, PACK], F32, name="step4")
         dsc4 = sb.tile([P, PACK], F32, name="dsc4")
         esc4 = sb.tile([P, PACK], F32, name="esc4")
@@ -58,6 +57,8 @@ def tile_attend_ownlists_delta_pl_kernel(tc, state, keys, vals, step, esc, dsc, 
         state_parts = [slice(0, 1), slice(1, 2), slice(2, 4)]
         for t in range(PACK):
             nc.sync.dma_start(key_pool[t][:], keys_planes[:, t, :])
+            if t == 0:
+                nc.sync.dma_start(offsets[:], offs)
             if t < len(state_parts):
                 nc.sync.dma_start(state_raw[:, state_parts[t], :], state_planes[:, state_parts[t], :])
         for t in range(PACK):
@@ -66,6 +67,9 @@ def tile_attend_ownlists_delta_pl_kernel(tc, state, keys, vals, step, esc, dsc, 
 
         ident = sb.tile([P, P], F32, name="ident")
         make_identity(nc, ident[:])
+
+        warm = sb.tile([P, 1], F32, name="warm")
+        nc.scalar.copy(warm[:], ident[:, 0:1])
 
         step_rows = bank(0, "step_rows")
         for r in range(PACK):
@@ -98,7 +102,7 @@ def tile_attend_ownlists_delta_pl_kernel(tc, state, keys, vals, step, esc, dsc, 
         state_scales = sb.tile([P, E], U8, name="state_scales", align_bytes=64)
         quantize(state_codes[:], state_scales[:], state_bf[:])
 
-        key_bf = sb.tile([P, I * PACK], BF16, name="key_bf", align_bytes=64)
+        key_bf = sb.tile([P, I * PACK], BF16, name="key_bf", tag="staging", align_bytes=64)
         nc.scalar.copy(key_bf[:].rearrange("p (c i t) -> p c t i", t=PACK, i=4),
                        kg[:].rearrange("p t (c i) -> p c t i", i=4))
         key_codes = sb.tile([P, I], U32, name="key_codes", align_bytes=64)
@@ -111,25 +115,31 @@ def tile_attend_ownlists_delta_pl_kernel(tc, state, keys, vals, step, esc, dsc, 
 
         es_bf = sb.tile([P, QUARTERS, PACK, QW // PACK, PACK], BF16, name="es_bf", align_bytes=64)
         esc_spread = esc4[:].unsqueeze(1).unsqueeze(1).to_broadcast([P, QUARTERS, QW // PACK, PACK])
+        pred_banks = [2, 3, 0, 1]
+        preds = []
         for t in range(PACK):
-            vg = sb.tile([P, I], F32, name="vg%d" % t)
-            nc.vector.tensor_copy(vg[:], val_pool[t][:].indirect(offsets[:]))
-            pred = bank(2 + t % 2, "pred%d" % t)
+            pred = bank(pred_banks[t], "pred%d" % t)
             cols = slice(P * t, P * (t + 1))
             mx(pred[:].rearrange("p a b -> p (a b)"), state_codes[:, cols], state_scales[:, cols],
                key_codes[:], key_scales[:])
+            preds.append(pred)
+        vg_first = sb.tile([P, I], F32, name="vg_first")
+        vg_rest = sb.tile([P, PACK - 1, I], F32, name="vg_rest", tag="staging", align_bytes=64)
+        for t in range(PACK):
+            vg = vg_first[:] if t == 0 else vg_rest[:, t - 1, :]
+            nc.vector.tensor_copy(vg, val_pool[t][:].indirect(offsets[:]))
             neg_pred = sb.tile([P, PACK, P], F32, name="neg_pred%d" % t)
             nc.scalar.activation(neg_pred[:],
-                                 pred[:].rearrange("p a b -> p (a b)").rearrange("p (s r) -> p r s", r=PACK),
+                                 preds[t][:].rearrange("p a b -> p (a b)").rearrange("p (s r) -> p r s", r=PACK),
                                  COPY, scale=-1.0)
+            val_dealt = sb.tile([P, PACK, P], F32, name="val_dealt%d" % t)
+            nc.scalar.copy(val_dealt[:].rearrange("p r (c i) -> p c r i", i=4),
+                           vg.rearrange("p (c i r) -> p c r i", i=4, r=PACK))
             err = bank(4 + t, "err%d" % t)
-            vals_first = t < 2
-            sides = [[vg[:, r:I:PACK] for r in range(PACK)], [neg_pred[:, r, :] for r in range(PACK)]]
-            if not vals_first:
-                sides = sides[::-1]
+            sides = [val_dealt, neg_pred] if t == 0 else [neg_pred, val_dealt]
             for k in range(2):
                 for r in range(PACK):
-                    nc.tensor.matmul(err[:, r, :], sides[k][r], ident[:], is_transpose=True,
+                    nc.tensor.matmul(err[:, r, :], sides[k][:, r, :], ident[:], is_transpose=True,
                                      start=(k == 0 and r == 0), stop=(k == 1 and r == PACK - 1))
             nc.vector.tensor_tensor(es_bf[:, :, t, :, :],
                                     err[:].rearrange("s r (q c) -> s q c r", q=QUARTERS),
@@ -139,6 +149,7 @@ def tile_attend_ownlists_delta_pl_kernel(tc, state, keys, vals, step, esc, dsc, 
         es_scales = sb.tile([P, E], U8, name="es_scales", align_bytes=64)
         y_codes = sb.tile([P, E], U32, name="y_codes", align_bytes=64)
         y_scales = sb.tile([P, E], U8, name="y_scales", align_bytes=64)
+        y_bf = sb.tile([P, QUARTERS, QW * PACK], BF16, name="y_bf", align_bytes=64)
         out_rows = out_0.rearrange("(p t) e -> p t e", t=PACK)
         out_words = out_1.rearrange("z p c r -> p (z c r)").bitcast(I32)
         for q in range(QUARTERS):
@@ -146,7 +157,7 @@ def tile_attend_ownlists_delta_pl_kernel(tc, state, keys, vals, step, esc, dsc, 
             quantize(es_codes[:, cols], es_scales[:, cols], es_bf[:, q].rearrange("s t c r -> s (t c r)"))
         for q in range(QUARTERS):
             cols = slice(QW * q, QW * (q + 1))
-            upd = bank(q, "upd%d" % q)
+            upd = bank(pred_banks[q], "upd%d" % q)
             for t in range(PACK):
                 rows = slice(P * t, P * (t + 1))
                 mx(upd[:, t, :], ks_codes[:, rows], ks_scales[:, rows], es_codes[:, cols], es_scales[:, cols])
@@ -155,10 +166,12 @@ def tile_attend_ownlists_delta_pl_kernel(tc, state, keys, vals, step, esc, dsc, 
                                     upd[:].rearrange("p t (j c) -> p t c j", j=PACK),
                                     own_sb[:, :, cols].rearrange("p t (c j) -> p t c j", j=PACK), MULT)
             nc.sync.dma_start(out_rows[:, :, cols], y[:])
-            y_bf = sb.tile([P, QW * PACK], BF16, name="y_bf%d" % q, align_bytes=64)
-            nc.scalar.copy(y_bf[:].rearrange("p (c i t) -> p c t i", t=PACK, i=4),
+            nc.scalar.copy(y_bf[:, q, :].rearrange("p (c i t) -> p c t i", t=PACK, i=4),
                            y[:].rearrange("p t (c i) -> p c t i", i=4))
-            quantize(y_codes[:, cols], y_scales[:, cols], y_bf[:])
+            if q > 0:
+                first = 0 if q == 1 else q
+                run = slice(QW * first, QW * (q + 1))
+                quantize(y_codes[:, run], y_scales[:, run], y_bf[:, first:q + 1, :].rearrange("p q n -> p (q n)"))
             if q % 2 == 1:
                 half = slice(QW * (q - 1), QW * (q + 1))
                 nc.scalar.dma_start(out_words[:, half], y_codes[:, half].bitcast(I32))

@@ -14,6 +14,7 @@ U16 = mybir.dt.uint16
 U8 = mybir.dt.uint8
 FP8X4 = mybir.dt.float8_e4m3fn_x4
 MULT = mybir.AluOpType.mult
+ADD = mybir.AluOpType.add
 COPY = mybir.ActivationFunctionType.Copy
 
 P = 128
@@ -46,23 +47,22 @@ def tile_attend_ownlists_delta_pl_kernel(tc, state, keys, vals, step, esc, dsc, 
         step4 = sb.tile([P, PACK], F32, name="step4")
         dsc4 = sb.tile([P, PACK], F32, name="dsc4")
         esc4 = sb.tile([P, PACK], F32, name="esc4")
-        nc.scalar.dma_start(step4[:], step.rearrange("(s r) o -> s (r o)", r=PACK))
-        nc.scalar.dma_start(dsc4[:], dsc.rearrange("o (p t) -> (o p) t", t=PACK))
-        nc.scalar.dma_start(esc4[:], esc.rearrange("(s r) o -> s (r o)", r=PACK))
+        nc.sync.dma_start(step4[:], step.rearrange("(s r) o -> s (r o)", r=PACK))
 
-        key_pool = [sb.tile([P, T], F32, name="key_pool%d" % t) for t in range(PACK)]
-        val_pool = [sb.tile([P, T], F32, name="val_pool%d" % t) for t in range(PACK)]
-        state_raw = sb.tile([P, PACK, E], F32, name="state_raw")
+        key_pool = [sb.tile([P, T], F32, name="key_pool%d" % t, tag="keys%d" % t, align_bytes=64) for t in range(PACK)]
+        val_pool = [sb.tile([P, T], F32, name="val_pool%d" % t, tag="vals%d" % t, align_bytes=64) for t in range(PACK)]
+        state_raw = [sb.tile([P, PACK, E // 2], F32, name="state_raw%d" % h) for h in range(2)]
         own_sb = sb.tile([P, PACK, E], F32, name="own_sb")
-        state_parts = [slice(0, 1), slice(1, 2), slice(2, 4)]
         for t in range(PACK):
             nc.sync.dma_start(key_pool[t][:], keys_planes[:, t, :])
             if t == 0:
                 nc.sync.dma_start(offsets[:], offs)
-            if t < len(state_parts):
-                nc.sync.dma_start(state_raw[:, state_parts[t], :], state_planes[:, state_parts[t], :])
+                nc.sync.dma_start(dsc4[:], dsc.rearrange("o (p t) -> (o p) t", t=PACK))
+        for h in range(2):
+            nc.sync.dma_start(state_raw[h][:], state_planes[:, :, h * E // 2:(h + 1) * E // 2])
         for t in range(PACK):
             nc.sync.dma_start(val_pool[t][:], vals_planes[:, t, :])
+        nc.sync.dma_start(esc4[:], esc.rearrange("(s r) o -> s (r o)", r=PACK))
         nc.sync.dma_start(own_sb[:], own.rearrange("(p t) e -> p t e", t=PACK))
 
         ident = sb.tile([P, P], F32, name="ident")
@@ -76,46 +76,50 @@ def tile_attend_ownlists_delta_pl_kernel(tc, state, keys, vals, step, esc, dsc, 
             nc.tensor.transpose(step_rows[:, r, :], step4[:, r:r + 1].to_broadcast([P, P]), ident[:])
 
         kg = sb.tile([P, PACK, I], F32, name="kg")
-        ks_rows = [sb.tile([P, I], BF16, name="ks_rows%d" % t, align_bytes=64) for t in range(PACK)]
-        ks_bf = sb.tile([P, D * PACK], BF16, name="ks_bf", align_bytes=64)
-        ks_words = ks_bf[:].bitcast(F32).rearrange("s (t p u) -> s t p u", t=PACK, u=2)
+        for t in range(PACK):
+            nc.vector.tensor_copy(kg[:, t, :], key_pool[t][:].indirect(offsets[:]))
+        ks_rows = sb.tile([P, PACK, I], BF16, name="ks_rows", tag="keys3", align_bytes=64)
+        turned = []
         for pair in range(2):
-            ks_turned = bank(1, "ks_turned%d" % pair)
+            ks_turned = bank(1 + pair, "ks_turned%d" % pair)
+            turned.append(ks_turned)
             for t in (2 * pair, 2 * pair + 1):
-                nc.vector.tensor_copy(kg[:, t, :], key_pool[t][:].indirect(offsets[:]))
                 nc.vector.scalar_tensor_tensor(
-                    out=ks_rows[t][:].rearrange("p (s r) -> p s r", r=PACK),
+                    out=ks_rows[:, t, :].rearrange("p (s r) -> p s r", r=PACK),
                     in0=kg[:, t, :].rearrange("p (s r) -> p s r", r=PACK),
                     scalar=dsc4[:, t:t + 1],
                     in1=step_rows[:].rearrange("p r s -> p s r"),
                     op0=MULT, op1=MULT)
-                words = ks_rows[t][:].bitcast(F32)
+                words = ks_rows[:, t, :].bitcast(F32)
                 for u in range(2):
                     nc.tensor.transpose(ks_turned[:, 2 * (t % 2) + u, :], words[:, u:I // 2:2], ident[:])
-            nc.scalar.copy(ks_words[:, 2 * pair:2 * pair + 2, :, :],
-                           ks_turned[:].rearrange("s (t u) p -> s t p u", u=2))
 
-        state_bf = sb.tile([P, E * PACK], BF16, name="state_bf", align_bytes=64)
-        nc.scalar.copy(state_bf[:].rearrange("p (t m j) -> p m j t", t=PACK, j=PACK),
-                       state_raw[:].rearrange("p j (m t) -> p m j t", t=PACK))
-        state_codes = sb.tile([P, E], U32, name="state_codes", align_bytes=64)
-        state_scales = sb.tile([P, E], U8, name="state_scales", align_bytes=64)
-        quantize(state_codes[:], state_scales[:], state_bf[:])
+        state_bf = sb.tile([P, E * PACK], BF16, name="state_bf", tag="staging", align_bytes=64)
+        state_dealt = state_bf[:].rearrange("p (t m j) -> p m t j", t=PACK, j=PACK)
 
-        key_bf = sb.tile([P, I * PACK], BF16, name="key_bf", tag="staging", align_bytes=64)
+        for h in range(2):
+            nc.gpsimd.tensor_scalar(state_dealt[:, h * P // 2:(h + 1) * P // 2, :, :],
+                                    state_raw[h][:].rearrange("p j (m t) -> p m t j", t=PACK),
+                                    1.0, 0.0, MULT, ADD)
+        key_bf = sb.tile([P, I * PACK], BF16, name="key_bf", align_bytes=64)
         nc.scalar.copy(key_bf[:].rearrange("p (c i t) -> p c t i", t=PACK, i=4),
                        kg[:].rearrange("p t (c i) -> p c t i", i=4))
         key_codes = sb.tile([P, I], U32, name="key_codes", align_bytes=64)
         key_scales = sb.tile([P, I], U8, name="key_scales", align_bytes=64)
         quantize(key_codes[:], key_scales[:], key_bf[:])
+        state_codes = sb.tile([P, E], U32, name="state_codes", align_bytes=64)
+        state_scales = sb.tile([P, E], U8, name="state_scales", align_bytes=64)
+        quantize(state_codes[:], state_scales[:], state_bf[:])
 
-        ks_codes = sb.tile([P, D], U32, name="ks_codes", align_bytes=64)
-        ks_scales = sb.tile([P, D], U8, name="ks_scales", align_bytes=64)
-        quantize(ks_codes[:], ks_scales[:], ks_bf[:])
+        ks_bf = sb.tile([P, D * PACK], BF16, name="ks_bf", align_bytes=64)
+        ks_words = ks_bf[:].bitcast(F32).rearrange("s (t p u) -> s t p u", t=PACK, u=2)
+        for pair in range(2):
+            nc.scalar.copy(ks_words[:, 2 * pair:2 * pair + 2, :, :],
+                           turned[pair][:].rearrange("s (t u) p -> s t p u", u=2))
 
         es_bf = sb.tile([P, QUARTERS, PACK, QW // PACK, PACK], BF16, name="es_bf", align_bytes=64)
         esc_spread = esc4[:].unsqueeze(1).unsqueeze(1).to_broadcast([P, QUARTERS, QW // PACK, PACK])
-        pred_banks = [2, 3, 0, 1]
+        pred_banks = [3, 0, 1, 2]
         preds = []
         for t in range(PACK):
             pred = bank(pred_banks[t], "pred%d" % t)
@@ -128,15 +132,20 @@ def tile_attend_ownlists_delta_pl_kernel(tc, state, keys, vals, step, esc, dsc, 
         for t in range(PACK):
             vg = vg_first[:] if t == 0 else vg_rest[:, t - 1, :]
             nc.vector.tensor_copy(vg, val_pool[t][:].indirect(offsets[:]))
-            neg_pred = sb.tile([P, PACK, P], F32, name="neg_pred%d" % t)
+            neg_pred = sb.tile([P, PACK, P], F32, name="neg_pred%d" % t, tag="neg%d" % t)
             nc.scalar.activation(neg_pred[:],
                                  preds[t][:].rearrange("p a b -> p (a b)").rearrange("p (s r) -> p r s", r=PACK),
                                  COPY, scale=-1.0)
-            val_dealt = sb.tile([P, PACK, P], F32, name="val_dealt%d" % t)
-            nc.scalar.copy(val_dealt[:].rearrange("p r (c i) -> p c r i", i=4),
-                           vg.rearrange("p (c i r) -> p c r i", i=4, r=PACK))
-            err = bank(4 + t, "err%d" % t)
+            if t < PACK - 1:
+                val_dealt = sb.tile([P, PACK, P], F32, name="val_dealt%d" % t, tag="neg%d" % (t - 1))
+                nc.scalar.copy(val_dealt[:].rearrange("p r (c i) -> p c r i", i=4),
+                               vg.rearrange("p (c i r) -> p c r i", i=4, r=PACK))
+            else:
+                val_dealt = sb.tile([P, PACK, P], F32, name="val_dealt%d" % t)
+                nc.gpsimd.tensor_scalar(val_dealt[:].rearrange("p r (c i) -> p c r i", i=4),
+                                        vg.rearrange("p (c i r) -> p c r i", i=4, r=PACK), 1.0, 0.0, MULT, ADD)
             sides = [val_dealt, neg_pred] if t == 0 else [neg_pred, val_dealt]
+            err = bank(4 + t, "err%d" % t)
             for k in range(2):
                 for r in range(PACK):
                     nc.tensor.matmul(err[:, r, :], sides[k][:, r, :], ident[:], is_transpose=True,
@@ -144,6 +153,10 @@ def tile_attend_ownlists_delta_pl_kernel(tc, state, keys, vals, step, esc, dsc, 
             nc.vector.tensor_tensor(es_bf[:, :, t, :, :],
                                     err[:].rearrange("s r (q c) -> s q c r", q=QUARTERS),
                                     esc_spread, MULT)
+
+        ks_codes = sb.tile([P, D], U32, name="ks_codes", tag="vals3", align_bytes=64)
+        ks_scales = sb.tile([P, D], U8, name="ks_scales", align_bytes=64)
+        quantize(ks_codes[:], ks_scales[:], ks_bf[:])
 
         es_codes = sb.tile([P, E], U32, name="es_codes", align_bytes=64)
         es_scales = sb.tile([P, E], U8, name="es_scales", align_bytes=64)
@@ -174,7 +187,8 @@ def tile_attend_ownlists_delta_pl_kernel(tc, state, keys, vals, step, esc, dsc, 
                 quantize(y_codes[:, run], y_scales[:, run], y_bf[:, first:q + 1, :].rearrange("p q n -> p (q n)"))
             if q % 2 == 1:
                 half = slice(QW * (q - 1), QW * (q + 1))
-                nc.scalar.dma_start(out_words[:, half], y_codes[:, half].bitcast(I32))
+                queue = nc.sync if q == 1 else nc.scalar
+                queue.dma_start(out_words[:, half], y_codes[:, half].bitcast(I32))
         out_scales = out_2.rearrange("z q c -> (z q) c").bitcast(I32)
         for quad in range(4):
             eng = nc.sync if quad % 2 == 0 else nc.scalar

@@ -19,8 +19,11 @@ COPY = mybir.ActivationFunctionType.Copy
 
 P = 128
 PACK = 4
+LAST = PACK - 1
+RUN = 4
 QUARTERS = 4
 QW = E // QUARTERS
+EARLY_PLANES = 2
 
 
 def tile_attend_ownlists_delta_pl_kernel(tc, state, keys, vals, step, esc, dsc, own, offs, out_0, out_1, out_2):
@@ -39,6 +42,9 @@ def tile_attend_ownlists_delta_pl_kernel(tc, state, keys, vals, step, esc, dsc, 
             nc.tensor.matmul_mx(out=out, lhsT=lhs.bitcast(FP8X4), lhsT_scale=lhs_scale,
                                 rhs=rhs.bitcast(FP8X4), rhs_scale=rhs_scale, start=True, stop=True)
 
+        def gpsimd_move(out, in_):
+            nc.gpsimd.tensor_scalar(out, in_, 1.0, 0.0, MULT, ADD)
+
         keys_planes = keys.rearrange("(p t) n -> p t n", t=PACK)
         vals_planes = vals.rearrange("(p t) n -> p t n", t=PACK)
         state_planes = state.rearrange("(p t) e -> p t e", t=PACK)
@@ -47,21 +53,23 @@ def tile_attend_ownlists_delta_pl_kernel(tc, state, keys, vals, step, esc, dsc, 
         step4 = sb.tile([P, PACK], F32, name="step4")
         dsc4 = sb.tile([P, PACK], F32, name="dsc4")
         esc4 = sb.tile([P, PACK], F32, name="esc4")
-        nc.sync.dma_start(step4[:], step.rearrange("(s r) o -> s (r o)", r=PACK))
-
-        key_pool = [sb.tile([P, T], F32, name="key_pool%d" % t, tag="keys%d" % t, align_bytes=64) for t in range(PACK)]
-        val_pool = [sb.tile([P, T], F32, name="val_pool%d" % t, tag="vals%d" % t, align_bytes=64) for t in range(PACK)]
-        state_raw = [sb.tile([P, PACK, E // 2], F32, name="state_raw%d" % h) for h in range(2)]
+        key_pool = [sb.tile([P, T], F32, name="key_pool%d" % t) for t in range(PACK)]
+        val_pool = [sb.tile([P, T], F32, name="val_pool%d" % t) for t in range(PACK)]
+        state_raw = [sb.tile([P, PACK, E // 2], F32, name="state_raw%d" % h, tag="half%d" % h, align_bytes=64)
+                     for h in range(2)]
         own_sb = sb.tile([P, PACK, E], F32, name="own_sb")
+
+        nc.sync.dma_start(step4[:], step.rearrange("(s r) o -> s (r o)", r=PACK))
         for t in range(PACK):
             nc.sync.dma_start(key_pool[t][:], keys_planes[:, t, :])
             if t == 0:
                 nc.sync.dma_start(offsets[:], offs)
                 nc.sync.dma_start(dsc4[:], dsc.rearrange("o (p t) -> (o p) t", t=PACK))
-        for h in range(2):
-            nc.sync.dma_start(state_raw[h][:], state_planes[:, :, h * E // 2:(h + 1) * E // 2])
         for t in range(PACK):
             nc.sync.dma_start(val_pool[t][:], vals_planes[:, t, :])
+            if t == EARLY_PLANES - 1:
+                for h in range(2):
+                    nc.sync.dma_start(state_raw[h][:], state_planes[:, :, h * E // 2:(h + 1) * E // 2])
         nc.sync.dma_start(esc4[:], esc.rearrange("(s r) o -> s (r o)", r=PACK))
         nc.sync.dma_start(own_sb[:], own.rearrange("(p t) e -> p t e", t=PACK))
 
@@ -74,36 +82,32 @@ def tile_attend_ownlists_delta_pl_kernel(tc, state, keys, vals, step, esc, dsc, 
         step_rows = bank(0, "step_rows")
         for r in range(PACK):
             nc.tensor.transpose(step_rows[:, r, :], step4[:, r:r + 1].to_broadcast([P, P]), ident[:])
+        step_by_slot = step_rows[:].rearrange("p r s -> p s r")
 
-        kg = sb.tile([P, PACK, I], F32, name="kg")
-        for t in range(PACK):
-            nc.vector.tensor_copy(kg[:, t, :], key_pool[t][:].indirect(offsets[:]))
-        ks_rows = sb.tile([P, PACK, I], BF16, name="ks_rows", tag="keys3", align_bytes=64)
-        turned = []
+        listed_keys = sb.tile([P, PACK, I], F32, name="listed_keys")
+        ks_turned = []
         for pair in range(2):
-            ks_turned = bank(1 + pair, "ks_turned%d" % pair)
-            turned.append(ks_turned)
+            turned = bank(1 + pair, "ks_turned%d" % pair)
+            ks_turned.append(turned)
             for t in (2 * pair, 2 * pair + 1):
-                nc.vector.scalar_tensor_tensor(
-                    out=ks_rows[:, t, :].rearrange("p (s r) -> p s r", r=PACK),
-                    in0=kg[:, t, :].rearrange("p (s r) -> p s r", r=PACK),
-                    scalar=dsc4[:, t:t + 1],
-                    in1=step_rows[:].rearrange("p r s -> p s r"),
-                    op0=MULT, op1=MULT)
-                words = ks_rows[:, t, :].bitcast(F32)
+                nc.vector.tensor_copy(listed_keys[:, t, :], key_pool[t][:].indirect(offsets[:]))
+                ks_rows = sb.tile([P, I], BF16, name="ks_rows%d" % t, align_bytes=64)
+                factor = sb.tile([P, I], F32, name="factor%d" % t)
+                nc.scalar.activation(factor[:].rearrange("p (s r) -> p s r", r=PACK), step_by_slot, COPY,
+                                     scale=dsc4[:, t:t + 1])
+                nc.gpsimd.tensor_tensor(ks_rows[:], listed_keys[:, t, :], factor[:], MULT)
+                slot_pairs = ks_rows[:].bitcast(F32)
                 for u in range(2):
-                    nc.tensor.transpose(ks_turned[:, 2 * (t % 2) + u, :], words[:, u:I // 2:2], ident[:])
+                    nc.tensor.transpose(turned[:, 2 * (t % 2) + u, :], slot_pairs[:, u:I // 2:2], ident[:])
 
-        state_bf = sb.tile([P, E * PACK], BF16, name="state_bf", tag="staging", align_bytes=64)
-        state_dealt = state_bf[:].rearrange("p (t m j) -> p m t j", t=PACK, j=PACK)
-
-        for h in range(2):
-            nc.gpsimd.tensor_scalar(state_dealt[:, h * P // 2:(h + 1) * P // 2, :, :],
-                                    state_raw[h][:].rearrange("p j (m t) -> p m t j", t=PACK),
-                                    1.0, 0.0, MULT, ADD)
         key_bf = sb.tile([P, I * PACK], BF16, name="key_bf", align_bytes=64)
-        nc.scalar.copy(key_bf[:].rearrange("p (c i t) -> p c t i", t=PACK, i=4),
-                       kg[:].rearrange("p t (c i) -> p c t i", i=4))
+        nc.scalar.copy(key_bf[:].rearrange("p (c n j) -> p c j n", j=PACK, n=RUN),
+                       listed_keys[:].rearrange("p j (c n) -> p c j n", n=RUN))
+        state_bf = sb.tile([P, E * PACK], BF16, name="state_bf", tag="staging", align_bytes=64)
+        state_dealt = state_bf[:].rearrange("p (t h m j) -> p h m t j", t=PACK, h=2, j=PACK)
+        state_walk = [half[:].rearrange("p j (m t) -> p m t j", t=PACK) for half in state_raw]
+        gpsimd_move(state_dealt[:, 0], state_walk[0])
+        nc.scalar.copy(state_dealt[:, 1], state_walk[1])
         key_codes = sb.tile([P, I], U32, name="key_codes", align_bytes=64)
         key_scales = sb.tile([P, I], U8, name="key_scales", align_bytes=64)
         quantize(key_codes[:], key_scales[:], key_bf[:])
@@ -111,50 +115,46 @@ def tile_attend_ownlists_delta_pl_kernel(tc, state, keys, vals, step, esc, dsc, 
         state_scales = sb.tile([P, E], U8, name="state_scales", align_bytes=64)
         quantize(state_codes[:], state_scales[:], state_bf[:])
 
-        ks_bf = sb.tile([P, D * PACK], BF16, name="ks_bf", align_bytes=64)
+        ks_bf = sb.tile([P, D * PACK], BF16, name="ks_bf", tag="half1", align_bytes=64)
         ks_words = ks_bf[:].bitcast(F32).rearrange("s (t p u) -> s t p u", t=PACK, u=2)
         for pair in range(2):
             nc.scalar.copy(ks_words[:, 2 * pair:2 * pair + 2, :, :],
-                           turned[pair][:].rearrange("s (t u) p -> s t p u", u=2))
+                           ks_turned[pair][:].rearrange("s (t u) p -> s t p u", u=2))
+
+        product_banks = [3, 0, 1, 2]
+        preds = []
+        for t in range(PACK):
+            pred = bank(product_banks[t], "pred%d" % t)[:].rearrange("p a b -> p (a b)")
+            tile_cols = slice(P * t, P * (t + 1))
+            mx(pred, state_codes[:, tile_cols], state_scales[:, tile_cols], key_codes[:], key_scales[:])
+            preds.append(pred)
 
         es_bf = sb.tile([P, QUARTERS, PACK, QW // PACK, PACK], BF16, name="es_bf", align_bytes=64)
         esc_spread = esc4[:].unsqueeze(1).unsqueeze(1).to_broadcast([P, QUARTERS, QW // PACK, PACK])
-        pred_banks = [3, 0, 1, 2]
-        preds = []
+        early_vals = sb.tile([P, EARLY_PLANES, I], F32, name="early_vals")
+        late_vals = sb.tile([P, PACK - EARLY_PLANES, I], F32, name="late_vals", tag="staging", align_bytes=64)
         for t in range(PACK):
-            pred = bank(pred_banks[t], "pred%d" % t)
-            cols = slice(P * t, P * (t + 1))
-            mx(pred[:].rearrange("p a b -> p (a b)"), state_codes[:, cols], state_scales[:, cols],
-               key_codes[:], key_scales[:])
-            preds.append(pred)
-        vg_first = sb.tile([P, I], F32, name="vg_first")
-        vg_rest = sb.tile([P, PACK - 1, I], F32, name="vg_rest", tag="staging", align_bytes=64)
-        for t in range(PACK):
-            vg = vg_first[:] if t == 0 else vg_rest[:, t - 1, :]
-            nc.vector.tensor_copy(vg, val_pool[t][:].indirect(offsets[:]))
-            neg_pred = sb.tile([P, PACK, P], F32, name="neg_pred%d" % t, tag="neg%d" % t)
-            nc.scalar.activation(neg_pred[:],
-                                 preds[t][:].rearrange("p a b -> p (a b)").rearrange("p (s r) -> p r s", r=PACK),
-                                 COPY, scale=-1.0)
-            if t < PACK - 1:
-                val_dealt = sb.tile([P, PACK, P], F32, name="val_dealt%d" % t, tag="neg%d" % (t - 1))
-                nc.scalar.copy(val_dealt[:].rearrange("p r (c i) -> p c r i", i=4),
-                               vg.rearrange("p (c i r) -> p c r i", i=4, r=PACK))
+            early = t < EARLY_PLANES
+            listed_vals = early_vals[:, t, :] if early else late_vals[:, t - EARLY_PLANES, :]
+            nc.vector.tensor_copy(listed_vals, val_pool[t][:].indirect(offsets[:]))
+            neg_pred = sb.tile([P, PACK, P], F32, name="neg_pred%d" % t)
+            nc.scalar.activation(neg_pred[:], preds[t].rearrange("p (s r) -> p r s", r=PACK), COPY, scale=-1.0)
+            if early:
+                sides = [listed_vals.rearrange("p (s r) -> p r s", r=PACK), neg_pred]
             else:
-                val_dealt = sb.tile([P, PACK, P], F32, name="val_dealt%d" % t)
-                nc.gpsimd.tensor_scalar(val_dealt[:].rearrange("p r (c i) -> p c r i", i=4),
-                                        vg.rearrange("p (c i r) -> p c r i", i=4, r=PACK), 1.0, 0.0, MULT, ADD)
-            sides = [val_dealt, neg_pred] if t == 0 else [neg_pred, val_dealt]
-            err = bank(4 + t, "err%d" % t)
-            for k in range(2):
+                vals_dealt = sb.tile([P, PACK, P], F32, name="vals_dealt%d" % t, tag="dealt%d" % t, align_bytes=64)
+                gpsimd_move(vals_dealt[:].rearrange("p r (c n) -> p c r n", n=RUN),
+                            listed_vals.rearrange("p (c n r) -> p c r n", n=RUN, r=PACK))
+                sides = [neg_pred, vals_dealt]
+            err = bank(PACK + t, "err%d" % t)
+            for k, side in enumerate(sides):
                 for r in range(PACK):
-                    nc.tensor.matmul(err[:, r, :], sides[k][:, r, :], ident[:], is_transpose=True,
-                                     start=(k == 0 and r == 0), stop=(k == 1 and r == PACK - 1))
-            nc.vector.tensor_tensor(es_bf[:, :, t, :, :],
-                                    err[:].rearrange("s r (q c) -> s q c r", q=QUARTERS),
+                    nc.tensor.matmul(err[:, r, :], side[:, r, :], ident[:], is_transpose=True,
+                                     start=(k == 0 and r == 0), stop=(k == 1 and r == LAST))
+            nc.vector.tensor_tensor(es_bf[:, :, t, :, :], err[:].rearrange("s r (q c) -> s q c r", q=QUARTERS),
                                     esc_spread, MULT)
 
-        ks_codes = sb.tile([P, D], U32, name="ks_codes", tag="vals3", align_bytes=64)
+        ks_codes = sb.tile([P, D], U32, name="ks_codes", tag="dealt%d" % EARLY_PLANES, align_bytes=64)
         ks_scales = sb.tile([P, D], U8, name="ks_scales", align_bytes=64)
         quantize(ks_codes[:], ks_scales[:], ks_bf[:])
 
@@ -162,7 +162,7 @@ def tile_attend_ownlists_delta_pl_kernel(tc, state, keys, vals, step, esc, dsc, 
         es_scales = sb.tile([P, E], U8, name="es_scales", align_bytes=64)
         y_codes = sb.tile([P, E], U32, name="y_codes", align_bytes=64)
         y_scales = sb.tile([P, E], U8, name="y_scales", align_bytes=64)
-        y_bf = sb.tile([P, QUARTERS, QW * PACK], BF16, name="y_bf", align_bytes=64)
+        y_bf = sb.tile([P, E, PACK], BF16, name="y_bf", align_bytes=64)
         out_rows = out_0.rearrange("(p t) e -> p t e", t=PACK)
         out_words = out_1.rearrange("z p c r -> p (z c r)").bitcast(I32)
         for q in range(QUARTERS):
@@ -170,26 +170,32 @@ def tile_attend_ownlists_delta_pl_kernel(tc, state, keys, vals, step, esc, dsc, 
             quantize(es_codes[:, cols], es_scales[:, cols], es_bf[:, q].rearrange("s t c r -> s (t c r)"))
         for q in range(QUARTERS):
             cols = slice(QW * q, QW * (q + 1))
-            upd = bank(pred_banks[q], "upd%d" % q)
+            update = bank(product_banks[q], "update%d" % q)
             for t in range(PACK):
-                rows = slice(P * t, P * (t + 1))
-                mx(upd[:, t, :], ks_codes[:, rows], ks_scales[:, rows], es_codes[:, cols], es_scales[:, cols])
+                tile_cols = slice(P * t, P * (t + 1))
+                mx(update[:, t, :], ks_codes[:, tile_cols], ks_scales[:, tile_cols],
+                   es_codes[:, cols], es_scales[:, cols])
             y = sb.tile([P, PACK, QW], F32, name="y%d" % q)
-            nc.vector.tensor_tensor(y[:].rearrange("p t (c j) -> p t c j", j=PACK),
-                                    upd[:].rearrange("p t (j c) -> p t c j", j=PACK),
-                                    own_sb[:, :, cols].rearrange("p t (c j) -> p t c j", j=PACK), MULT)
+            pieces = 2 if q == QUARTERS - 1 else 1
+            width = QW // pieces
+            for piece in range(pieces):
+                part = slice(width * piece, width * (piece + 1))
+                groups = slice(part.start // PACK, part.stop // PACK)
+                whole = slice(cols.start + part.start, cols.start + part.stop)
+                nc.vector.tensor_tensor(y[:, :, part].rearrange("p t (c j) -> p t c j", j=PACK),
+                                        update[:].rearrange("p t (j c) -> p t c j", j=PACK)[:, :, groups, :],
+                                        own_sb[:, :, whole].rearrange("p t (c j) -> p t c j", j=PACK), MULT)
+                nc.scalar.copy(y_bf[:, whole, :].rearrange("p (c n) t -> p c t n", n=RUN),
+                               y[:, :, part].rearrange("p t (c n) -> p c t n", n=RUN))
+                if q > 0:
+                    ready = slice(0 if q == 1 else whole.start, whole.stop)
+                    quantize(y_codes[:, ready], y_scales[:, ready], y_bf[:, ready, :].rearrange("p c t -> p (c t)"))
             nc.sync.dma_start(out_rows[:, :, cols], y[:])
-            nc.scalar.copy(y_bf[:, q, :].rearrange("p (c i t) -> p c t i", t=PACK, i=4),
-                           y[:].rearrange("p t (c i) -> p c t i", i=4))
-            if q > 0:
-                first = 0 if q == 1 else q
-                run = slice(QW * first, QW * (q + 1))
-                quantize(y_codes[:, run], y_scales[:, run], y_bf[:, first:q + 1, :].rearrange("p q n -> p (q n)"))
             if q % 2 == 1:
                 half = slice(QW * (q - 1), QW * (q + 1))
                 queue = nc.sync if q == 1 else nc.scalar
                 queue.dma_start(out_words[:, half], y_codes[:, half].bitcast(I32))
         out_scales = out_2.rearrange("z q c -> (z q) c").bitcast(I32)
         for quad in range(4):
-            eng = nc.sync if quad % 2 == 0 else nc.scalar
-            eng.dma_start(out_scales[4 * quad:4 * quad + 4, :], y_scales[32 * quad:32 * quad + 4, :].bitcast(I32))
+            queue = nc.sync if quad % 2 == 0 else nc.scalar
+            queue.dma_start(out_scales[4 * quad:4 * quad + 4, :], y_scales[32 * quad:32 * quad + 4, :].bitcast(I32))

from contextlib import ExitStack

import concourse.mybir as mybir
from concourse.masks import make_identity

D, T, I, E = 512, 1024, 512, 512
FLOPS = 2 * D * E * I * 2

F32 = mybir.dt.float32
BF16 = mybir.dt.bfloat16
I32 = mybir.dt.int32
U32 = mybir.dt.uint32
U16 = mybir.dt.uint16
U8 = mybir.dt.uint8
FP8X4 = mybir.dt.float8_e4m3fn_x4
MULT = mybir.AluOpType.mult
ADD = mybir.AluOpType.add
COPY = mybir.ActivationFunctionType.Copy

P = 128
PACK = 4
LAST = PACK - 1
RUN = 4
QUARTERS = 4
QW = E // QUARTERS
EARLY_PLANES = 2


def tile_attend_ownlists_delta_pl_kernel(tc, state, keys, vals, step, esc, dsc, own, offs, out_0, out_1, out_2):
    nc = tc.nc
    with ExitStack() as ctx:
        sb = ctx.enter_context(tc.tile_pool(name="sb", bufs=1))
        ps = ctx.enter_context(tc.psum_pool(name="ps", bufs=1))

        def bank(n, name):
            return ps.tile([P, PACK, P], F32, name=name, tag="bank%d" % n)

        def quantize(codes, scales, values):
            nc.vector.quantize_mx(out=codes.bitcast(FP8X4), scales=scales, in_=values)

        def mx(out, lhs, lhs_scale, rhs, rhs_scale):
            nc.tensor.matmul_mx(out=out, lhsT=lhs.bitcast(FP8X4), lhsT_scale=lhs_scale,
                                rhs=rhs.bitcast(FP8X4), rhs_scale=rhs_scale, start=True, stop=True)

        def gpsimd_move(out, in_):
            nc.gpsimd.tensor_scalar(out, in_, 1.0, 0.0, MULT, ADD)

        keys_planes = keys.rearrange("(p t) n -> p t n", t=PACK)
        vals_planes = vals.rearrange("(p t) n -> p t n", t=PACK)
        state_planes = state.rearrange("(p t) e -> p t e", t=PACK)

        offsets = sb.tile([P, I // 16], U16, name="offsets")
        step4 = sb.tile([P, PACK], F32, name="step4")
        dsc4 = sb.tile([P, PACK], F32, name="dsc4")
        esc4 = sb.tile([P, PACK], F32, name="esc4")
        key_pool = [sb.tile([P, T], F32, name="key_pool%d" % t) for t in range(PACK)]
        val_pool = [sb.tile([P, T], F32, name="val_pool%d" % t) for t in range(PACK)]
        state_raw = [sb.tile([P, PACK, E // 2], F32, name="state_raw%d" % h, tag="half%d" % h, align_bytes=64)
                     for h in range(2)]
        own_sb = sb.tile([P, PACK, E], F32, name="own_sb")

        nc.sync.dma_start(step4[:], step.rearrange("(s r) o -> s (r o)", r=PACK))
        for t in range(PACK):
            nc.sync.dma_start(key_pool[t][:], keys_planes[:, t, :])
            if t == 0:
                nc.sync.dma_start(offsets[:], offs)
                nc.sync.dma_start(dsc4[:], dsc.rearrange("o (p t) -> (o p) t", t=PACK))
        for t in range(PACK):
            nc.sync.dma_start(val_pool[t][:], vals_planes[:, t, :])
            if t == EARLY_PLANES - 1:
                for h in range(2):
                    nc.sync.dma_start(state_raw[h][:], state_planes[:, :, h * E // 2:(h + 1) * E // 2])
        nc.sync.dma_start(esc4[:], esc.rearrange("(s r) o -> s (r o)", r=PACK))
        nc.sync.dma_start(own_sb[:], own.rearrange("(p t) e -> p t e", t=PACK))

        ident = sb.tile([P, P], F32, name="ident")
        make_identity(nc, ident[:])

        warm = sb.tile([P, 1], F32, name="warm")
        nc.scalar.copy(warm[:], ident[:, 0:1])

        step_rows = bank(0, "step_rows")
        for r in range(PACK):
            nc.tensor.transpose(step_rows[:, r, :], step4[:, r:r + 1].to_broadcast([P, P]), ident[:])
        step_by_slot = step_rows[:].rearrange("p r s -> p s r")

        listed_keys = sb.tile([P, PACK, I], F32, name="listed_keys")
        ks_turned = []
        for pair in range(2):
            turned = bank(1 + pair, "ks_turned%d" % pair)
            ks_turned.append(turned)
            for t in (2 * pair, 2 * pair + 1):
                nc.vector.tensor_copy(listed_keys[:, t, :], key_pool[t][:].indirect(offsets[:]))
                ks_rows = sb.tile([P, I], BF16, name="ks_rows%d" % t, align_bytes=64)
                factor = sb.tile([P, I], F32, name="factor%d" % t)
                nc.scalar.activation(factor[:].rearrange("p (s r) -> p s r", r=PACK), step_by_slot, COPY,
                                     scale=dsc4[:, t:t + 1])
                nc.gpsimd.tensor_tensor(ks_rows[:], listed_keys[:, t, :], factor[:], MULT)
                slot_pairs = ks_rows[:].bitcast(F32)
                for u in range(2):
                    nc.tensor.transpose(turned[:, 2 * (t % 2) + u, :], slot_pairs[:, u:I // 2:2], ident[:])

        key_bf = sb.tile([P, I * PACK], BF16, name="key_bf", align_bytes=64)
        nc.scalar.copy(key_bf[:].rearrange("p (c n j) -> p c j n", j=PACK, n=RUN),
                       listed_keys[:].rearrange("p j (c n) -> p c j n", n=RUN))
        state_bf = sb.tile([P, E * PACK], BF16, name="state_bf", tag="staging", align_bytes=64)
        state_dealt = state_bf[:].rearrange("p (t h m j) -> p h m t j", t=PACK, h=2, j=PACK)
        state_walk = [half[:].rearrange("p j (m t) -> p m t j", t=PACK) for half in state_raw]
        gpsimd_move(state_dealt[:, 0], state_walk[0])
        nc.scalar.copy(state_dealt[:, 1], state_walk[1])
        key_codes = sb.tile([P, I], U32, name="key_codes", align_bytes=64)
        key_scales = sb.tile([P, I], U8, name="key_scales", align_bytes=64)
        quantize(key_codes[:], key_scales[:], key_bf[:])
        state_codes = sb.tile([P, E], U32, name="state_codes", align_bytes=64)
        state_scales = sb.tile([P, E], U8, name="state_scales", align_bytes=64)
        quantize(state_codes[:], state_scales[:], state_bf[:])

        ks_bf = sb.tile([P, D * PACK], BF16, name="ks_bf", tag="half1", align_bytes=64)
        ks_words = ks_bf[:].bitcast(F32).rearrange("s (t p u) -> s t p u", t=PACK, u=2)
        for pair in range(2):
            nc.scalar.copy(ks_words[:, 2 * pair:2 * pair + 2, :, :],
                           ks_turned[pair][:].rearrange("s (t u) p -> s t p u", u=2))

        product_banks = [3, 0, 1, 2]
        preds = []
        for t in range(PACK):
            pred = bank(product_banks[t], "pred%d" % t)[:].rearrange("p a b -> p (a b)")
            tile_cols = slice(P * t, P * (t + 1))
            mx(pred, state_codes[:, tile_cols], state_scales[:, tile_cols], key_codes[:], key_scales[:])
            preds.append(pred)

        es_bf = sb.tile([P, QUARTERS, PACK, QW // PACK, PACK], BF16, name="es_bf", align_bytes=64)
        esc_spread = esc4[:].unsqueeze(1).unsqueeze(1).to_broadcast([P, QUARTERS, QW // PACK, PACK])
        early_vals = sb.tile([P, EARLY_PLANES, I], F32, name="early_vals")
        late_vals = sb.tile([P, PACK - EARLY_PLANES, I], F32, name="late_vals", tag="staging", align_bytes=64)
        for t in range(PACK):
            early = t < EARLY_PLANES
            listed_vals = early_vals[:, t, :] if early else late_vals[:, t - EARLY_PLANES, :]
            nc.vector.tensor_copy(listed_vals, val_pool[t][:].indirect(offsets[:]))
            neg_pred = sb.tile([P, PACK, P], F32, name="neg_pred%d" % t)
            nc.scalar.activation(neg_pred[:], preds[t].rearrange("p (s r) -> p r s", r=PACK), COPY, scale=-1.0)
            if early:
                sides = [listed_vals.rearrange("p (s r) -> p r s", r=PACK), neg_pred]
            else:
                vals_dealt = sb.tile([P, PACK, P], F32, name="vals_dealt%d" % t, tag="dealt%d" % t, align_bytes=64)
                gpsimd_move(vals_dealt[:].rearrange("p r (c n) -> p c r n", n=RUN),
                            listed_vals.rearrange("p (c n r) -> p c r n", n=RUN, r=PACK))
                sides = [neg_pred, vals_dealt]
            err = bank(PACK + t, "err%d" % t)
            for k, side in enumerate(sides):
                for r in range(PACK):
                    nc.tensor.matmul(err[:, r, :], side[:, r, :], ident[:], is_transpose=True,
                                     start=(k == 0 and r == 0), stop=(k == 1 and r == LAST))
            nc.vector.tensor_tensor(es_bf[:, :, t, :, :], err[:].rearrange("s r (q c) -> s q c r", q=QUARTERS),
                                    esc_spread, MULT)

        ks_codes = sb.tile([P, D], U32, name="ks_codes", tag="dealt%d" % EARLY_PLANES, align_bytes=64)
        ks_scales = sb.tile([P, D], U8, name="ks_scales", align_bytes=64)
        quantize(ks_codes[:], ks_scales[:], ks_bf[:])

        es_codes = sb.tile([P, E], U32, name="es_codes", align_bytes=64)
        es_scales = sb.tile([P, E], U8, name="es_scales", align_bytes=64)
        y_codes = sb.tile([P, E], U32, name="y_codes", align_bytes=64)
        y_scales = sb.tile([P, E], U8, name="y_scales", align_bytes=64)
        y_bf = sb.tile([P, E, PACK], BF16, name="y_bf", align_bytes=64)
        out_rows = out_0.rearrange("(p t) e -> p t e", t=PACK)
        out_words = out_1.rearrange("z p c r -> p (z c r)").bitcast(I32)
        for q in range(QUARTERS):
            cols = slice(QW * q, QW * (q + 1))
            quantize(es_codes[:, cols], es_scales[:, cols], es_bf[:, q].rearrange("s t c r -> s (t c r)"))
        for q in range(QUARTERS):
            cols = slice(QW * q, QW * (q + 1))
            update = bank(product_banks[q], "update%d" % q)
            for t in range(PACK):
                tile_cols = slice(P * t, P * (t + 1))
                mx(update[:, t, :], ks_codes[:, tile_cols], ks_scales[:, tile_cols],
                   es_codes[:, cols], es_scales[:, cols])
            y = sb.tile([P, PACK, QW], F32, name="y%d" % q)
            pieces = 2 if q == QUARTERS - 1 else 1
            width = QW // pieces
            for piece in range(pieces):
                part = slice(width * piece, width * (piece + 1))
                groups = slice(part.start // PACK, part.stop // PACK)
                whole = slice(cols.start + part.start, cols.start + part.stop)
                nc.vector.tensor_tensor(y[:, :, part].rearrange("p t (c j) -> p t c j", j=PACK),
                                        update[:].rearrange("p t (j c) -> p t c j", j=PACK)[:, :, groups, :],
                                        own_sb[:, :, whole].rearrange("p t (c j) -> p t c j", j=PACK), MULT)
                nc.scalar.copy(y_bf[:, whole, :].rearrange("p (c n) t -> p c t n", n=RUN),
                               y[:, :, part].rearrange("p t (c n) -> p c t n", n=RUN))
                if q > 0:
                    ready = slice(0 if q == 1 else whole.start, whole.stop)
                    quantize(y_codes[:, ready], y_scales[:, ready], y_bf[:, ready, :].rearrange("p c t -> p (c t)"))
            nc.sync.dma_start(out_rows[:, :, cols], y[:])
            if q % 2 == 1:
                half = slice(QW * (q - 1), QW * (q + 1))
                queue = nc.sync if q == 1 else nc.scalar
                queue.dma_start(out_words[:, half], y_codes[:, half].bitcast(I32))
        out_scales = out_2.rearrange("z q c -> (z q) c").bitcast(I32)
        for quad in range(4):
            queue = nc.sync if quad % 2 == 0 else nc.scalar
            queue.dma_start(out_scales[4 * quad:4 * quad + 4, :], y_scales[32 * quad:32 * quad + 4, :].bitcast(I32))
